import numpy as np
import ml_dtypes


def mxq(x, axis, fmt="e4m3"):
    dtype, down = {"e4m3": (ml_dtypes.float8_e4m3fn, 7), "e5m2": (ml_dtypes.float8_e5m2, 14)}[fmt]
    v = np.moveaxis(np.asarray(x, np.float32).astype(ml_dtypes.bfloat16).astype(np.float64), axis, -1)
    blocks = v.reshape(v.shape[:-1] + (-1, 32))
    amax = np.abs(blocks).max(-1, keepdims=True)
    byte = np.maximum(np.where(amax > 0, np.frexp(amax)[1] - 1 + 127, 0) - down, 1)
    scale = np.exp2(byte - 127.0)
    codes = (blocks / scale).astype(np.float32).astype(dtype).astype(np.float64)
    return np.moveaxis((codes * scale).reshape(v.shape), -1, axis)


WIDE = False


def mx_kscale(k):
    if not WIDE:
        return np.ones(k)
    levels = np.array([10, -10, 5, -5, 0])
    if k % 512:
        return np.exp2(np.random.permutation(np.resize(levels, k // 32))).repeat(32)
    a = np.empty((k // 512, 16))
    for p in range(k // 512):
        a[p, :8] = np.random.permutation(np.resize(levels, 8))
        for g in range(8):
            far = levels[np.abs(levels - a[p, g]) >= 10]
            a[p, g + 8] = far[np.random.randint(len(far))]
    return np.exp2(a.ravel()).repeat(32)


def f64(x):
    return np.asarray(x).astype(np.float64)


def striped(idx):
    return np.tile(idx.reshape(-1, 16).T, (8, 1)).astype(np.uint16)


def unstriped(offs):
    return offs[:16].T.reshape(-1).astype(np.int64)


def pack_weight(w):
    k, n = w.shape
    w = f64(np.asarray(w, np.float32).astype(ml_dtypes.bfloat16)).reshape(k // 32, 32, n)
    amax = np.abs(w).max(1)
    byte = np.clip(np.where(amax > 0, np.frexp(amax)[1] - 1 + 127 - 7, 1), 1, 254)
    scaled = (w * np.exp2(127.0 - byte)[:, None, :]).reshape(k, n).astype(np.float32)
    words = np.ascontiguousarray(scaled.reshape(k // 512, 128, 4, n).transpose(0, 1, 3, 2)).astype(ml_dtypes.float8_e4m3fn).view(np.uint8)
    return words, np.ascontiguousarray(byte.astype(np.uint8).reshape(k // 512, 16, n))


def unpack_weight(words, scales):
    g, p, n, _ = words.shape
    vals = np.ascontiguousarray(words).view(ml_dtypes.float8_e4m3fn).astype(np.float64) * np.repeat(np.exp2(scales.astype(np.float64) - 127.0), 8, axis=1)[..., None]
    return vals.transpose(0, 1, 3, 2).reshape(g * 512, n)


def gelu(v):
    return 0.5 * v * (1.0 + np.tanh(np.sqrt(2.0 / np.pi) * (v + 0.044715 * v**3)))


K, T, S, H, N = 512, 2048, 1024, 512, 256
P = 2 ** 7


def setup_inputs():
    n = np.random.standard_normal
    s = mx_kscale(K)[:, None]
    u = mx_kscale(H)
    packed_w2 = pack_weight(n((H, N)) / np.sqrt(H) / u[:, None])
    return {
        "xT": (n((K, T)) * s).astype(np.float32),
        "w1": (n((K, H)) / np.sqrt(K) / s * u).astype(np.float32),
        "w2_words": packed_w2[0],
        "w2_scales": packed_w2[1],
        "share": np.tile(np.random.uniform(0.1, 0.9, S), (P, 1)).astype(np.float32),
        "offs": striped(np.random.permutation(T)[:S]),
        "par": striped(np.random.permutation(S)[(S * np.random.uniform(0, 1, S) ** 4).astype(np.int64)]),
    }


def reference(xT, w1, w2_words, w2_scales, share, offs, par):
    xq = mxq(f64(xT)[:, unstriped(offs)], 0, "e4m3")
    h = gelu(mxq(f64(w1), 0, "e4m3").T @ xq)
    z = h + h[:, unstriped(par)] * f64(share)[:1]
    return unpack_weight(w2_words, w2_scales).T @ mxq(z, 0, "e4m3")

@@ -1,0 +1,267 @@
+from contextlib import ExitStack
+
+import concourse.mybir as mybir
+from concourse.masks import make_identity
+
+K, T, S, H, N = 512, 2048, 1024, 512, 256
+FLOPS = 2 * S * H * (K + N)
+
+F32 = mybir.dt.float32
+BF16 = mybir.dt.bfloat16
+I32 = mybir.dt.int32
+U32 = mybir.dt.uint32
+U16 = mybir.dt.uint16
+U8 = mybir.dt.uint8
+FP8X4 = mybir.dt.float8_e4m3fn_x4
+GELU = mybir.ActivationFunctionType.Gelu_apprx_tanh
+MULT = mybir.AluOpType.mult
+ADD = mybir.AluOpType.add
+
+P = 128
+PACK = 4
+BANK = 512
+HALF = S // 2
+X_CHUNKS = (512, 512, 512, 256, 256)
+X_ON_VECTOR = (320, 320, 320, 160, 160)
+PICK_PIECES = (512, 256, 256)
+Z_PIECES = (256, 256, 256, 128, 128)
+USE_PE = True
+
+
+def spans(widths):
+    found, start = [], 0
+    for width in widths:
+        found.append((start, start + width))
+        start = start + width
+    return found
+
+
+def tile_picked_treeup_gelu_e_kernel(tc, xT, w1, w2_words, w2_scales, share, offs, par, out):
+    nc = tc.nc
+    with ExitStack() as ctx:
+        keep = ctx.enter_context(tc.tile_pool(name="keep", bufs=1))
+        psum = ctx.enter_context(tc.psum_pool(name="psum", bufs=4))
+
+        offs_sb = keep.tile([P, S // 16], U16, name="offs_sb")
+        par_sb = keep.tile([P, S // 16], U16, name="par_sb")
+
+        x_rows = xT.rearrange("(p j) c -> p j c", j=PACK)
+        x_raw = []
+        for c, (lo, hi) in enumerate(spans(X_CHUNKS)):
+            raw = keep.tile([P, PACK, hi - lo], F32, name="x_raw%d" % c)
+            nc.sync.dma_start(out=raw[:], in_=x_rows[:, :, lo:hi])
+            x_raw.append(raw)
+        nc.sync.dma_start(offs_sb[:], offs)
+        w1_raw = []
+        for n in range(2):
+            raw = keep.tile([P, PACK, H // 2], F32, name="w1_raw%d" % n)
+            nc.sync.dma_start(out=raw[:], in_=w1.rearrange("(p j) c -> p j c", j=PACK)[:, :, n * H // 2 : (n + 1) * H // 2])
+            w1_raw.append(raw)
+        nc.sync.dma_start(par_sb[:], par)
+        share_sb = []
+        for n in range(2):
+            part = keep.tile([P, HALF], F32, name="share%d" % n, tag="share%d" % n)
+            nc.sync.dma_start(out=part[:], in_=share[:, n * HALF : (n + 1) * HALF])
+            share_sb.append(part)
+        w2_codes = keep.tile([P, N], I32, name="w2_codes", align_bytes=64)
+        nc.sync.dma_start(out=w2_codes[:], in_=w2_words[0].rearrange("p n t -> p (n t)").bitcast(I32))
+        w2_plane = keep.tile([P, N], U8, name="w2_plane", align_bytes=64)
+        nc.vector.memset(w2_plane[:].bitcast(I32), 0)
+        for q in range(4):
+            nc.sync.dma_start(out=w2_plane[32 * q : 32 * q + 4, :].bitcast(I32), in_=w2_scales[0, 4 * q : 4 * q + 4, :].bitcast(I32))
+
+        zero = keep.tile([P, 1], F32, name="zero")
+        nc.vector.memset(zero[:], 0.0)
+        no_bias = keep.tile([P, 1], F32, name="no_bias")
+        nc.scalar.activation(no_bias[:], zero[:], GELU)
+        identity = keep.tile([P, P], F32, name="identity")
+        if USE_PE:
+            make_identity(nc, identity[:])
+
+        x_words = keep.tile([P, T], U32, name="x_words", align_bytes=64)
+        x_plane = keep.tile([P, T], U8, name="x_plane", align_bytes=64)
+        nc.vector.memset(x_plane[:].bitcast(I32), 0)
+        for c, (lo, hi) in enumerate(spans(X_CHUNKS)):
+            woven = keep.tile([P, hi - lo, PACK], BF16, name="x_woven%d" % c, align_bytes=64)
+            cut = X_ON_VECTOR[c]
+            if cut > 0:
+                nc.vector.tensor_copy(
+                    out=woven[:, 0:cut, :].rearrange("p (c i) t -> p c t i", i=4),
+                    in_=x_raw[c][:, :, 0:cut].rearrange("p t (c i) -> p c t i", i=4),
+                )
+            if cut < hi - lo:
+                nc.scalar.copy(
+                    out=woven[:, cut:, :].rearrange("p (c i) t -> p c t i", i=4),
+                    in_=x_raw[c][:, :, cut:].rearrange("p t (c i) -> p c t i", i=4),
+                )
+            nc.vector.quantize_mx(
+                out=x_words[:, lo:hi].bitcast(FP8X4), scales=x_plane[:, lo:hi], in_=woven[:].rearrange("p c t -> p (c t)")
+            )
+
+        picked = []
+
+        def pick(n):
+            lo, hi = spans(PICK_PIECES)[n]
+            words = keep.tile([P, hi - lo], U32, name="picked_words%d" % n, tag="turn%d" % (n - 1), align_bytes=64)
+            plane = keep.tile([P, hi - lo], U8, name="picked_plane%d" % n, align_bytes=64)
+            nc.vector.tensor_copy(words[:], x_words[:].indirect(offs_sb[:, lo // 16 : hi // 16]))
+            nc.vector.tensor_copy(plane[:], x_plane[:].indirect(offs_sb[:, lo // 16 : hi // 16]))
+            picked.append((words, plane))
+
+        w1_q = []
+        w1_woven = [keep.tile([P, 2, P, PACK], BF16, name="w1_woven%d" % u, tag="turn%d" % (u + 1), align_bytes=64) for u in range(2)]
+        for u in range(2):
+            for n in range(2):
+                nc.scalar.copy(
+                    out=w1_woven[u][:, :, n * P // 2 : (n + 1) * P // 2, :].rearrange("p e m j -> p m j e"),
+                    in_=w1_raw[n][:].rearrange("p j (m u e) -> p u m j e", u=2, e=2)[:, u],
+                )
+
+        def quantise_w1(u):
+            words = keep.tile([P, 2 * P], U32, name="w1_words%d" % u, align_bytes=64)
+            plane = keep.tile([P, 2 * P], U8, name="w1_plane%d" % u, align_bytes=64)
+            nc.vector.quantize_mx(out=words[:].bitcast(FP8X4), scales=plane[:], in_=w1_woven[u][:].rearrange("p e m j -> p (e m j)"))
+            for e in range(2):
+                w1_q.append((words[:, e * P : (e + 1) * P], plane[:, e * P : (e + 1) * P]))
+
+        h_window = [keep.tile([P, S], F32, name="h_window%d" % t) for t in range(PACK)]
+        h_half = [keep.tile([P, PACK, HALF], F32, name="h_half%d" % n) for n in range(2)]
+
+        def first_product(t, pieces):
+            acc = psum.tile([P, BANK], F32, name="acc")
+            first = spans(PICK_PIECES)[pieces[0]][0]
+            for n in pieces:
+                lo, hi = spans(PICK_PIECES)[n]
+                nc.tensor.matmul_mx(
+                    out=acc[:, lo - first : hi - first],
+                    lhsT=w1_q[t][0].bitcast(FP8X4), lhsT_scale=w1_q[t][1],
+                    rhs=picked[n][0][:].bitcast(FP8X4), rhs_scale=picked[n][1][:],
+                    start=True, stop=True,
+                )
+            last = spans(PICK_PIECES)[pieces[-1]][1]
+            nc.scalar.activation(h_window[t][:, first:last], acc[:, 0 : last - first], GELU, bias=no_bias[:])
+
+        def second_copy(t):
+            for n in range(1 if USE_PE else 0, 2):
+                nc.sync.dma_start(out=h_half[n][:, t, :], in_=h_window[t][:, n * HALF : (n + 1) * HALF])
+
+        pick(0)
+        pick(1)
+        quantise_w1(0)
+        pick(2)
+        quantise_w1(1)
+        first_product(0, [0])
+        first_product(0, [1])
+        first_product(1, [0])
+        first_product(0, [2])
+        second_copy(0)
+        first_product(1, [1, 2])
+        second_copy(1)
+        for t in range(2, PACK):
+            first_product(t, [0])
+            first_product(t, [1, 2])
+            second_copy(t)
+
+        taken = []
+
+        def take(t, n):
+            nc.vector.tensor_tensor(
+                taken[n][:, t, :], h_window[t][:].indirect(par_sb[:, n * HALF // 16 : (n + 1) * HALF // 16]), share_sb[n][:], MULT
+            )
+
+        z_woven = {}
+
+        def woven_tile(n):
+            lo, hi = spans(Z_PIECES)[n]
+            z_woven[n] = keep.tile([P, hi - lo, PACK], BF16, name="z_woven%d" % n, tag="z%d" % (n % 2 if n < 4 else n), align_bytes=64)
+            return z_woven[n]
+
+        def add(n):
+            lo, hi = spans(Z_PIECES)[n]
+            half, lo, hi = lo // HALF, lo % HALF, (hi - 1) % HALF + 1
+            nc.vector.tensor_tensor(
+                woven_tile(n)[:].rearrange("p (c i) t -> p c t i", i=4),
+                taken[half][:, :, lo:hi].rearrange("p t (c i) -> p c t i", i=4),
+                h_half[half][:, :, lo:hi].rearrange("p t (c i) -> p c t i", i=4),
+                ADD,
+            )
+
+        out_rows = out.rearrange("(u p) c -> p u c", p=P)
+
+        def second_product(n):
+            lo, hi = spans(Z_PIECES)[n]
+            width = hi - lo
+            words = keep.tile([P, width], U32, name="z_words%d" % n, align_bytes=64)
+            plane = keep.tile([P, width], U8, name="z_plane%d" % n, align_bytes=64)
+            nc.vector.quantize_mx(out=words[:].bitcast(FP8X4), scales=plane[:], in_=z_woven[n][:].rearrange("p c t -> p (c t)"))
+            result = keep.tile([P, N // P, width], F32, name="result%d" % n)
+            last = n == len(Z_PIECES) - 1
+            acc = psum.tile([P, N // P, width], F32, name="acc")
+            for u in range(N // P):
+                if last and u == 1:
+                    acc = psum.tile([P, N // P, width], F32, name="acc")
+                nc.tensor.matmul_mx(
+                    out=acc[:, u, :],
+                    lhsT=w2_codes[:, u * P : (u + 1) * P].bitcast(FP8X4), lhsT_scale=w2_plane[:, u * P : (u + 1) * P],
+                    rhs=words[:].bitcast(FP8X4), rhs_scale=plane[:],
+                    start=True, stop=True,
+                )
+                if last and u == 0:
+                    nc.scalar.copy(out=result[:, 0, :], in_=acc[:, 0, :])
+                if last and u == 1:
+                    nc.vector.tensor_copy(out=result[:, 1, :], in_=acc[:, 1, :])
+            if not last:
+                nc.scalar.copy(out=result[:], in_=acc[:])
+            nc.sync.dma_start(out=out_rows[:, :, lo:hi], in_=result[:])
+
+        taken.append(keep.tile([P, PACK, HALF], F32, name="taken0"))
+        if USE_PE:
+            sums = [psum.tile([P, PACK, P], F32, name="sums%d" % j, tag="sums") for j in range(HALF // P)]
+            for t in range(PACK):
+                take(t, 0)
+                for j in range(HALF // P):
+                    cols = slice(j * P, (j + 1) * P)
+                    nc.tensor.matmul(sums[j][:, t, :], h_window[t][:, cols], identity[:], start=True, stop=False, is_transpose=True)
+                    nc.tensor.matmul(sums[j][:, t, :], taken[0][:, t, cols], identity[:], start=False, stop=True, is_transpose=True)
+            for n in range(2):
+                back = psum.tile([P, 2, 2, P], F32, name="acc")
+                for jj in range(2):
+                    j = 2 * n + jj
+                    turned = keep.tile([P, 2, P, 2], BF16, name="turned%d" % j)
+                    nc.scalar.copy(out=turned[:], in_=sums[j][:].rearrange("q (u e) p -> q u p e", e=2))
+                    pairs = turned[:].rearrange("q u p e -> q (u p e)").bitcast(F32)
+                    for u in range(2):
+                        nc.tensor.transpose(back[:, jj, u, :], pairs[:, u * P : (u + 1) * P], identity[:])
+                nc.scalar.copy(
+                    out=woven_tile(n)[:].rearrange("p c t -> p (c t)").bitcast(F32).rearrange("p (j c u) -> p j c u", j=2, u=2),
+                    in_=back[:].rearrange("p j u c -> p j c u"),
+                )
+            taken.append(keep.tile([P, PACK, HALF], F32, name="taken1", tag="share0"))
+            for t in range(PACK):
+                take(t, 1)
+            second_product(0)
+            add(2)
+            second_product(1)
+            add(3)
+            second_product(2)
+            add(4)
+            second_product(3)
+            second_product(4)
+        else:
+            for t in range(PACK):
+                take(t, 0)
+            taken.append(keep.tile([P, PACK, HALF], F32, name="taken1", tag="share0"))
+            take(0, 1)
+            add(0)
+            take(1, 1)
+            add(1)
+            second_product(0)
+            take(2, 1)
+            second_product(1)
+            take(3, 1)
+            add(2)
+            add(3)
+            second_product(2)
+            add(4)
+            second_product(3)
+            second_product(4)

@@ -21,9 +21,12 @@ P = 128
 PACK = 4
 BANK = 512
 HALF = S // 2
-X_CHUNKS = (512, 512, 512, 256, 256)
-X_ON_VECTOR = (320, 320, 320, 160, 160)
-PICK_PIECES = (512, 256, 256)
+ON_PE = 640
+TAKES = (ON_PE, S - ON_PE)
+X_CHUNKS = ((1024, 1024), (1024, 512, 512))
+X_ON_VECTOR = ((640, 640), (0, 512, 320))
+W1_CHUNKS = (192, 320)
+PICK_PIECES = (256, 256, 256, 256)
 Z_PIECES = (256, 256, 256, 128, 128)
 USE_PE = True
 
@@ -40,28 +43,30 @@ def tile_picked_treeup_gelu_e_kernel(tc, xT, w1, w2_words, w2_scales, share, off
     nc = tc.nc
     with ExitStack() as ctx:
         keep = ctx.enter_context(tc.tile_pool(name="keep", bufs=1))
-        psum = ctx.enter_context(tc.psum_pool(name="psum", bufs=4))
+        psum = ctx.enter_context(tc.psum_pool(name="psum", bufs=1))
 
         offs_sb = keep.tile([P, S // 16], U16, name="offs_sb")
         par_sb = keep.tile([P, S // 16], U16, name="par_sb")
 
-        x_rows = xT.rearrange("(p j) c -> p j c", j=PACK)
+        x_rows = xT.rearrange("(p u e) c -> p u e c", u=2, e=2)
         x_raw = []
-        for c, (lo, hi) in enumerate(spans(X_CHUNKS)):
-            raw = keep.tile([P, PACK, hi - lo], F32, name="x_raw%d" % c)
-            nc.sync.dma_start(out=raw[:], in_=x_rows[:, :, lo:hi])
-            x_raw.append(raw)
-        nc.sync.dma_start(offs_sb[:], offs)
+        for u in range(2):
+            for c, (lo, hi) in enumerate(spans(X_CHUNKS[u])):
+                raw = keep.tile([P, 2, hi - lo], F32, name="x_raw%d_%d" % (u, c))
+                nc.sync.dma_start(out=raw[:], in_=x_rows[:, u, :, lo:hi])
+                x_raw.append((u, lo, hi, X_ON_VECTOR[u][c], raw))
+                if u == 0 and c == 0:
+                    nc.sync.dma_start(offs_sb[:], offs)
         w1_raw = []
-        for n in range(2):
-            raw = keep.tile([P, PACK, H // 2], F32, name="w1_raw%d" % n)
-            nc.sync.dma_start(out=raw[:], in_=w1.rearrange("(p j) c -> p j c", j=PACK)[:, :, n * H // 2 : (n + 1) * H // 2])
+        for n, (lo, hi) in enumerate(spans(W1_CHUNKS)):
+            raw = keep.tile([P, PACK, hi - lo], F32, name="w1_raw%d" % n, tag="w1_raw%d" % n, align_bytes=64)
+            nc.sync.dma_start(out=raw[:], in_=w1.rearrange("(p j) c -> p j c", j=PACK)[:, :, lo:hi])
             w1_raw.append(raw)
         nc.sync.dma_start(par_sb[:], par)
         share_sb = []
-        for n in range(2):
-            part = keep.tile([P, HALF], F32, name="share%d" % n, tag="share%d" % n)
-            nc.sync.dma_start(out=part[:], in_=share[:, n * HALF : (n + 1) * HALF])
+        for n, (lo, hi) in enumerate(spans(TAKES)):
+            part = keep.tile([P, hi - lo], F32, name="share%d" % n, tag="share%d" % n)
+            nc.sync.dma_start(out=part[:], in_=share[:, lo:hi])
             share_sb.append(part)
         w2_codes = keep.tile([P, N], I32, name="w2_codes", align_bytes=64)
         nc.sync.dma_start(out=w2_codes[:], in_=w2_words[0].rearrange("p n t -> p (n t)").bitcast(I32))
@@ -78,42 +83,73 @@ def tile_picked_treeup_gelu_e_kernel(tc, xT, w1, w2_words, w2_scales, share, off
         if USE_PE:
             make_identity(nc, identity[:])
 
-        x_words = keep.tile([P, T], U32, name="x_words", align_bytes=64)
-        x_plane = keep.tile([P, T], U8, name="x_plane", align_bytes=64)
-        nc.vector.memset(x_plane[:].bitcast(I32), 0)
-        for c, (lo, hi) in enumerate(spans(X_CHUNKS)):
-            woven = keep.tile([P, hi - lo, PACK], BF16, name="x_woven%d" % c, align_bytes=64)
-            cut = X_ON_VECTOR[c]
+        x_pairs = [keep.tile([P, T, 2], BF16, name="x_pairs%d" % u) for u in range(2)]
+        gathered = [keep.tile([P, 2, hi - lo], U32, name="gathered%d" % n) for n, (lo, hi) in enumerate(spans(PICK_PIECES))]
+
+        def cast(u, lo, hi, cut, raw):
             if cut > 0:
                 nc.vector.tensor_copy(
-                    out=woven[:, 0:cut, :].rearrange("p (c i) t -> p c t i", i=4),
-                    in_=x_raw[c][:, :, 0:cut].rearrange("p t (c i) -> p c t i", i=4),
+                    out=x_pairs[u][:, lo : lo + cut, :].rearrange("p (c i) e -> p c e i", i=4),
+                    in_=raw[:, :, 0:cut].rearrange("p e (c i) -> p c e i", i=4),
                 )
             if cut < hi - lo:
                 nc.scalar.copy(
-                    out=woven[:, cut:, :].rearrange("p (c i) t -> p c t i", i=4),
-                    in_=x_raw[c][:, :, cut:].rearrange("p t (c i) -> p c t i", i=4),
+                    out=x_pairs[u][:, lo + cut : hi, :].rearrange("p (c i) e -> p c e i", i=4),
+                    in_=raw[:, :, cut:].rearrange("p e (c i) -> p c e i", i=4),
                 )
-            nc.vector.quantize_mx(
-                out=x_words[:, lo:hi].bitcast(FP8X4), scales=x_plane[:, lo:hi], in_=woven[:].rearrange("p c t -> p (c t)")
-            )
 
-        picked = []
-
-        def pick(n):
+        def gather(u, n):
             lo, hi = spans(PICK_PIECES)[n]
-            words = keep.tile([P, hi - lo], U32, name="picked_words%d" % n, tag="turn%d" % (n - 1), align_bytes=64)
+            window = x_pairs[u][:].rearrange("p c e -> p (c e)").bitcast(U32)
+            nc.vector.tensor_copy(gathered[n][:, u, :], window.indirect(offs_sb[:, lo // 16 : hi // 16]))
+
+        x_woven = {}
+        x_halves = []
+
+        def weave(n):
+            lo, hi = spans(PICK_PIECES)[n]
+            if n < 3:
+                x_halves.append(keep.tile([P, HALF, 2], U32, name="x_woven%d" % n, tag=("turn0", "w1_raw1", "turn1")[n], align_bytes=64))
+            x_woven[n] = x_halves[-1][:, (n // 3) * (hi - lo) : (n // 3 + 1) * (hi - lo), :]
+            if n < 2:
+                nc.scalar.copy(
+                    out=x_woven[n].rearrange("p (c i) u -> p c u i", i=2),
+                    in_=gathered[n][:].rearrange("p u (c i) -> p c u i", i=2),
+                )
+            else:
+                nc.vector.tensor_copy(
+                    out=x_woven[n].bitcast(I32).rearrange("p (c i) u -> p c u i", i=2),
+                    in_=gathered[n][:].bitcast(I32).rearrange("p u (c i) -> p c u i", i=2),
+                )
+
+        picked = {}
+
+        def quantise_x(n):
+            lo, hi = spans(PICK_PIECES)[n]
+            words = keep.tile([P, hi - lo], U32, name="picked_words%d" % n, align_bytes=64)
             plane = keep.tile([P, hi - lo], U8, name="picked_plane%d" % n, align_bytes=64)
-            nc.vector.tensor_copy(words[:], x_words[:].indirect(offs_sb[:, lo // 16 : hi // 16]))
-            nc.vector.tensor_copy(plane[:], x_plane[:].indirect(offs_sb[:, lo // 16 : hi // 16]))
-            picked.append((words, plane))
+            nc.vector.quantize_mx(
+                out=words[:].bitcast(FP8X4), scales=plane[:], in_=x_woven[n].rearrange("p c u -> p (c u)").bitcast(BF16)
+            )
+            picked[n] = (words, plane)
+
+        for piece in x_raw:
+            if piece[0] == 0:
+                cast(*piece)
+        for n in range(4):
+            gather(0, n)
+        for piece in x_raw:
+            if piece[0] == 1:
+                cast(*piece)
 
         w1_q = []
-        w1_woven = [keep.tile([P, 2, P, PACK], BF16, name="w1_woven%d" % u, tag="turn%d" % (u + 1), align_bytes=64) for u in range(2)]
-        for u in range(2):
-            for n in range(2):
+        w1_woven = [keep.tile([P, 2, P, PACK], BF16, name="w1_woven%d" % u, tag="turn%d" % (1 + 2 * u), align_bytes=64) for u in range(2)]
+
+        def cast_w1(n):
+            lo, hi = spans(W1_CHUNKS)[n]
+            for u in range(2):
                 nc.scalar.copy(
-                    out=w1_woven[u][:, :, n * P // 2 : (n + 1) * P // 2, :].rearrange("p e m j -> p m j e"),
+                    out=w1_woven[u][:, :, lo // PACK : hi // PACK, :].rearrange("p e m j -> p m j e"),
                     in_=w1_raw[n][:].rearrange("p j (m u e) -> p u m j e", u=2, e=2)[:, u],
                 )
 
@@ -125,10 +161,13 @@ def tile_picked_treeup_gelu_e_kernel(tc, xT, w1, w2_words, w2_scales, share, off
                 w1_q.append((words[:, e * P : (e + 1) * P], plane[:, e * P : (e + 1) * P]))
 
         h_window = [keep.tile([P, S], F32, name="h_window%d" % t) for t in range(PACK)]
-        h_half = [keep.tile([P, PACK, HALF], F32, name="h_half%d" % n) for n in range(2)]
+        h_rest = keep.tile([P, PACK, S - ON_PE], F32, name="h_rest")
 
-        def first_product(t, pieces):
-            acc = psum.tile([P, BANK], F32, name="acc")
+        def bank(b, shape):
+            return psum.tile(shape, F32, name="bank%d" % b, tag="bank%d" % b)
+
+        def first_product(t, pieces, b):
+            acc = bank(b, [P, BANK])
             first = spans(PICK_PIECES)[pieces[0]][0]
             for n in pieces:
                 lo, hi = spans(PICK_PIECES)[n]
@@ -142,126 +181,132 @@ def tile_picked_treeup_gelu_e_kernel(tc, xT, w1, w2_words, w2_scales, share, off
             nc.scalar.activation(h_window[t][:, first:last], acc[:, 0 : last - first], GELU, bias=no_bias[:])
 
         def second_copy(t):
-            for n in range(1 if USE_PE else 0, 2):
-                nc.sync.dma_start(out=h_half[n][:, t, :], in_=h_window[t][:, n * HALF : (n + 1) * HALF])
+            nc.sync.dma_start(out=h_rest[:, t, :], in_=h_window[t][:, ON_PE : S])
 
-        pick(0)
-        pick(1)
+        cast_w1(0)
+        gather(1, 0)
+        weave(0)
+        cast_w1(1)
+        gather(1, 1)
+        weave(1)
+        gather(1, 2)
+        gather(1, 3)
+        quantise_x(0)
         quantise_w1(0)
-        pick(2)
+        weave(2)
+        weave(3)
+        quantise_x(2)
+        quantise_x(3)
+        quantise_x(1)
         quantise_w1(1)
-        first_product(0, [0])
-        first_product(0, [1])
-        first_product(1, [0])
-        first_product(0, [2])
+        first_product(0, [0], 0)
+        first_product(0, [2], 1)
+        first_product(0, [3], 2)
+        first_product(0, [1], 3)
         second_copy(0)
-        first_product(1, [1, 2])
+        first_product(1, [0, 1], 4)
+        first_product(1, [2, 3], 1)
         second_copy(1)
         for t in range(2, PACK):
-            first_product(t, [0])
-            first_product(t, [1, 2])
+            first_product(t, [0, 1], 2 * t + 1)
+            first_product(t, [2, 3], 6 if t == 2 else 0)
             second_copy(t)
 
-        taken = []
+        taken = {}
+        sums = {}
+        back_banks = (7, 0, 2)
+        sum_banks = ((2, 3, 4), (1, 5, 6))
 
         def take(t, n):
-            nc.vector.tensor_tensor(
-                taken[n][:, t, :], h_window[t][:].indirect(par_sb[:, n * HALF // 16 : (n + 1) * HALF // 16]), share_sb[n][:], MULT
-            )
+            lo, hi = spans(TAKES)[n]
+            nc.vector.tensor_tensor(taken[n][:, t, :], h_window[t][:].indirect(par_sb[:, lo // 16 : hi // 16]), share_sb[n][:], MULT)
+
+        def sum_up(t):
+            u, e = divmod(t, 2)
+            for j in range(ON_PE // P):
+                n, jj = divmod(j, 2)
+                if (u, n) not in sums:
+                    sums[u, n] = bank(sum_banks[u][n], [P, 2, 2, P])
+                cols = slice(j * P, (j + 1) * P)
+                nc.tensor.matmul(sums[u, n][:, jj, e, :], h_window[t][:, cols], identity[:], start=True, stop=False, is_transpose=True)
+                nc.tensor.matmul(sums[u, n][:, jj, e, :], taken[0][:, t, cols], identity[:], start=False, stop=True, is_transpose=True)
 
         z_woven = {}
 
         def woven_tile(n):
             lo, hi = spans(Z_PIECES)[n]
-            z_woven[n] = keep.tile([P, hi - lo, PACK], BF16, name="z_woven%d" % n, tag="z%d" % (n % 2 if n < 4 else n), align_bytes=64)
+            if n not in z_woven:
+                z_woven[n] = keep.tile([P, hi - lo, PACK], BF16, name="z_woven%d" % n, tag=("z0", "z1", "turned1_0", "z1", "turned1_0")[n], align_bytes=64)
             return z_woven[n]
 
         def add(n):
-            lo, hi = spans(Z_PIECES)[n]
-            half, lo, hi = lo // HALF, lo % HALF, (hi - 1) % HALF + 1
+            first, hi = spans(Z_PIECES)[n]
+            lo = max(first, ON_PE)
             nc.vector.tensor_tensor(
-                woven_tile(n)[:].rearrange("p (c i) t -> p c t i", i=4),
-                taken[half][:, :, lo:hi].rearrange("p t (c i) -> p c t i", i=4),
-                h_half[half][:, :, lo:hi].rearrange("p t (c i) -> p c t i", i=4),
+                woven_tile(n)[:, lo - first :, :].rearrange("p (c i) t -> p c t i", i=4),
+                taken[1][:, :, lo - ON_PE : hi - ON_PE].rearrange("p t (c i) -> p c t i", i=4),
+                h_rest[:, :, lo - ON_PE : hi - ON_PE].rearrange("p t (c i) -> p c t i", i=4),
                 ADD,
             )
 
+        back = {}
+
+        def turn_back(u, n):
+            lo, hi = spans(Z_PIECES)[n]
+            count = (min(hi, ON_PE) - lo) // P
+            if u == 0:
+                back[n] = bank(back_banks[n], [P, count, 2, P])
+            turned = keep.tile([P, count, P, 2], BF16, name="turned%d_%d" % (u, n), tag="turned%d_%d" % (u, n), align_bytes=64)
+            nc.scalar.copy(out=turned[:], in_=sums[u, n][:, 0:count].rearrange("q j e p -> q j p e"))
+            pairs = turned[:].rearrange("q j p e -> q (j p e)").bitcast(F32)
+            for jj in range(count):
+                nc.tensor.transpose(back[n][:, jj, u, :], pairs[:, jj * P : (jj + 1) * P], identity[:])
+            if u == 1:
+                nc.scalar.copy(
+                    out=woven_tile(n)[:, 0 : count * P, :].rearrange("p c t -> p (c t)").bitcast(F32).rearrange("p (j c u) -> p j c u", j=count, u=2),
+                    in_=back[n][:].rearrange("p j u c -> p j c u"),
+                )
+
         out_rows = out.rearrange("(u p) c -> p u c", p=P)
 
-        def second_product(n):
+        def second_product(n, banks, engines):
             lo, hi = spans(Z_PIECES)[n]
             width = hi - lo
             words = keep.tile([P, width], U32, name="z_words%d" % n, align_bytes=64)
             plane = keep.tile([P, width], U8, name="z_plane%d" % n, align_bytes=64)
             nc.vector.quantize_mx(out=words[:].bitcast(FP8X4), scales=plane[:], in_=z_woven[n][:].rearrange("p c t -> p (c t)"))
             result = keep.tile([P, N // P, width], F32, name="result%d" % n)
-            last = n == len(Z_PIECES) - 1
-            acc = psum.tile([P, N // P, width], F32, name="acc")
+            accs = [bank(b, [P, N // P, width]) for b in banks]
             for u in range(N // P):
-                if last and u == 1:
-                    acc = psum.tile([P, N // P, width], F32, name="acc")
                 nc.tensor.matmul_mx(
-                    out=acc[:, u, :],
+                    out=accs[u % len(banks)][:, u, :],
                     lhsT=w2_codes[:, u * P : (u + 1) * P].bitcast(FP8X4), lhsT_scale=w2_plane[:, u * P : (u + 1) * P],
                     rhs=words[:].bitcast(FP8X4), rhs_scale=plane[:],
                     start=True, stop=True,
                 )
-                if last and u == 0:
-                    nc.scalar.copy(out=result[:, 0, :], in_=acc[:, 0, :])
-                if last and u == 1:
-                    nc.vector.tensor_copy(out=result[:, 1, :], in_=acc[:, 1, :])
-            if not last:
-                nc.scalar.copy(out=result[:], in_=acc[:])
+            if len(banks) == 1:
+                engines[0](out=result[:], in_=accs[0][:])
+            else:
+                for u in range(N // P):
+                    engines[u](out=result[:, u, :], in_=accs[u][:, u, :])
             nc.sync.dma_start(out=out_rows[:, :, lo:hi], in_=result[:])
 
-        taken.append(keep.tile([P, PACK, HALF], F32, name="taken0"))
-        if USE_PE:
-            sums = [psum.tile([P, PACK, P], F32, name="sums%d" % j, tag="sums") for j in range(HALF // P)]
-            for t in range(PACK):
-                take(t, 0)
-                for j in range(HALF // P):
-                    cols = slice(j * P, (j + 1) * P)
-                    nc.tensor.matmul(sums[j][:, t, :], h_window[t][:, cols], identity[:], start=True, stop=False, is_transpose=True)
-                    nc.tensor.matmul(sums[j][:, t, :], taken[0][:, t, cols], identity[:], start=False, stop=True, is_transpose=True)
-            for n in range(2):
-                back = psum.tile([P, 2, 2, P], F32, name="acc")
-                for jj in range(2):
-                    j = 2 * n + jj
-                    turned = keep.tile([P, 2, P, 2], BF16, name="turned%d" % j)
-                    nc.scalar.copy(out=turned[:], in_=sums[j][:].rearrange("q (u e) p -> q u p e", e=2))
-                    pairs = turned[:].rearrange("q u p e -> q (u p e)").bitcast(F32)
-                    for u in range(2):
-                        nc.tensor.transpose(back[:, jj, u, :], pairs[:, u * P : (u + 1) * P], identity[:])
-                nc.scalar.copy(
-                    out=woven_tile(n)[:].rearrange("p c t -> p (c t)").bitcast(F32).rearrange("p (j c u) -> p j c u", j=2, u=2),
-                    in_=back[:].rearrange("p j u c -> p j c u"),
-                )
-            taken.append(keep.tile([P, PACK, HALF], F32, name="taken1", tag="share0"))
-            for t in range(PACK):
-                take(t, 1)
-            second_product(0)
-            add(2)
-            second_product(1)
-            add(3)
-            second_product(2)
-            add(4)
-            second_product(3)
-            second_product(4)
-        else:
-            for t in range(PACK):
-                take(t, 0)
-            taken.append(keep.tile([P, PACK, HALF], F32, name="taken1", tag="share0"))
-            take(0, 1)
-            add(0)
-            take(1, 1)
-            add(1)
-            second_product(0)
-            take(2, 1)
-            second_product(1)
-            take(3, 1)
-            add(2)
-            add(3)
-            second_product(2)
-            add(4)
-            second_product(3)
-            second_product(4)
+        taken[0] = keep.tile([P, PACK, TAKES[0]], F32, name="taken0")
+        for t in range(PACK):
+            take(t, 0)
+            sum_up(t)
+            if t % 2 == 1:
+                for n in range(len(back_banks)):
+                    turn_back(t // 2, n)
+        taken[1] = keep.tile([P, PACK, TAKES[1]], F32, name="taken1", tag="share0")
+        for t in range(PACK):
+            take(t, 1)
+        scalar, vector = nc.scalar.copy, nc.vector.tensor_copy
+        second_product(0, [3], [scalar])
+        add(2)
+        second_product(1, [4], [scalar])
+        second_product(2, [1], [scalar])
+        add(3)
+        add(4)
+        second_product(3, [5], [vector])
+        second_product(4, [6, 7], [scalar, vector])

@@ -19,16 +19,21 @@ ADD = mybir.AluOpType.add
 
 P = 128
 PACK = 4
-BANK = 512
-HALF = S // 2
-ON_PE = 640
-TAKES = (ON_PE, S - ON_PE)
+STRIPE = 16
+RUN = 4
+PIECE = 256
+PIECES = S // PIECE
+
 X_CHUNKS = ((1024, 1024), (1024, 512, 512))
 X_ON_VECTOR = ((640, 640), (0, 512, 320))
 W1_CHUNKS = (192, 320)
-PICK_PIECES = (256, 256, 256, 256)
-Z_PIECES = (256, 256, 256, 128, 128)
-USE_PE = True
+ON_TENSOR = 3 * PIECE
+NODE_PARTS = (ON_TENSOR, S - ON_TENSOR)
+Z_PIECES = (PIECE, PIECE, PIECE, P, P)
+
+SUM_BANKS = ((2, 3, 4), (1, 5, 6))
+BACK_BANKS = (7, 0, 2)
+OUT_BANKS = (3, 4, 1, 5, 6)
 
 
 def spans(widths):
@@ -45,268 +50,231 @@ def tile_picked_treeup_gelu_e_kernel(tc, xT, w1, w2_words, w2_scales, share, off
         keep = ctx.enter_context(tc.tile_pool(name="keep", bufs=1))
         psum = ctx.enter_context(tc.psum_pool(name="psum", bufs=1))
 
-        offs_sb = keep.tile([P, S // 16], U16, name="offs_sb")
-        par_sb = keep.tile([P, S // 16], U16, name="par_sb")
+        def bank(number, shape):
+            return psum.tile(shape, F32, name="bank%d" % number, tag="bank%d" % number)
 
+        def quantise(name, woven):
+            columns = woven.shape[1] // PACK
+            codes = keep.tile([P, columns], U32, name=name + "_codes", align_bytes=64)
+            scales = keep.tile([P, columns], U8, name=name + "_scales", align_bytes=64)
+            nc.vector.quantize_mx(out=codes[:].bitcast(FP8X4), scales=scales[:], in_=woven)
+            return codes, scales
+
+        offs_sb = keep.tile([P, S // STRIPE], U16, name="offs_sb")
+        par_sb = keep.tile([P, S // STRIPE], U16, name="par_sb")
         x_rows = xT.rearrange("(p u e) c -> p u e c", u=2, e=2)
-        x_raw = []
+        x_raw = {}
         for u in range(2):
             for c, (lo, hi) in enumerate(spans(X_CHUNKS[u])):
-                raw = keep.tile([P, 2, hi - lo], F32, name="x_raw%d_%d" % (u, c))
-                nc.sync.dma_start(out=raw[:], in_=x_rows[:, u, :, lo:hi])
-                x_raw.append((u, lo, hi, X_ON_VECTOR[u][c], raw))
-                if u == 0 and c == 0:
+                x_raw[u, c] = keep.tile([P, 2, hi - lo], F32, name="x_raw%d_%d" % (u, c))
+                nc.sync.dma_start(out=x_raw[u, c][:], in_=x_rows[:, u, :, lo:hi])
+                if (u, c) == (0, 0):
                     nc.sync.dma_start(offs_sb[:], offs)
+        w1_rows = w1.rearrange("(p j) c -> p j c", j=PACK)
         w1_raw = []
-        for n, (lo, hi) in enumerate(spans(W1_CHUNKS)):
-            raw = keep.tile([P, PACK, hi - lo], F32, name="w1_raw%d" % n, tag="w1_raw%d" % n, align_bytes=64)
-            nc.sync.dma_start(out=raw[:], in_=w1.rearrange("(p j) c -> p j c", j=PACK)[:, :, lo:hi])
-            w1_raw.append(raw)
+        for c, (lo, hi) in enumerate(spans(W1_CHUNKS)):
+            w1_raw.append(keep.tile([P, PACK, hi - lo], F32, name="w1_raw%d" % c, tag="w1_raw%d" % c, align_bytes=64))
+            nc.sync.dma_start(out=w1_raw[c][:], in_=w1_rows[:, :, lo:hi])
         nc.sync.dma_start(par_sb[:], par)
         share_sb = []
-        for n, (lo, hi) in enumerate(spans(TAKES)):
-            part = keep.tile([P, hi - lo], F32, name="share%d" % n, tag="share%d" % n)
-            nc.sync.dma_start(out=part[:], in_=share[:, lo:hi])
-            share_sb.append(part)
+        for part, (lo, hi) in enumerate(spans(NODE_PARTS)):
+            share_sb.append(keep.tile([P, hi - lo], F32, name="share%d" % part, tag="share%d" % part))
+            nc.sync.dma_start(out=share_sb[part][:], in_=share[:, lo:hi])
         w2_codes = keep.tile([P, N], I32, name="w2_codes", align_bytes=64)
         nc.sync.dma_start(out=w2_codes[:], in_=w2_words[0].rearrange("p n t -> p (n t)").bitcast(I32))
-        w2_plane = keep.tile([P, N], U8, name="w2_plane", align_bytes=64)
-        nc.vector.memset(w2_plane[:].bitcast(I32), 0)
+        w2_bytes = keep.tile([P, N], U8, name="w2_bytes", align_bytes=64)
+        nc.vector.memset(w2_bytes[:].bitcast(I32), 0)
         for q in range(4):
-            nc.sync.dma_start(out=w2_plane[32 * q : 32 * q + 4, :].bitcast(I32), in_=w2_scales[0, 4 * q : 4 * q + 4, :].bitcast(I32))
+            nc.sync.dma_start(out=w2_bytes[32 * q : 32 * q + 4, :].bitcast(I32), in_=w2_scales[0, 4 * q : 4 * q + 4, :].bitcast(I32))
 
         zero = keep.tile([P, 1], F32, name="zero")
         nc.vector.memset(zero[:], 0.0)
         no_bias = keep.tile([P, 1], F32, name="no_bias")
         nc.scalar.activation(no_bias[:], zero[:], GELU)
         identity = keep.tile([P, P], F32, name="identity")
-        if USE_PE:
-            make_identity(nc, identity[:])
+        make_identity(nc, identity[:])
 
         x_pairs = [keep.tile([P, T, 2], BF16, name="x_pairs%d" % u) for u in range(2)]
-        gathered = [keep.tile([P, 2, hi - lo], U32, name="gathered%d" % n) for n, (lo, hi) in enumerate(spans(PICK_PIECES))]
+        gathered = [keep.tile([P, 2, PIECE], U32, name="gathered%d" % n) for n in range(PIECES)]
 
-        def cast(u, lo, hi, cut, raw):
-            if cut > 0:
-                nc.vector.tensor_copy(
-                    out=x_pairs[u][:, lo : lo + cut, :].rearrange("p (c i) e -> p c e i", i=4),
-                    in_=raw[:, :, 0:cut].rearrange("p e (c i) -> p c e i", i=4),
-                )
-            if cut < hi - lo:
-                nc.scalar.copy(
-                    out=x_pairs[u][:, lo + cut : hi, :].rearrange("p (c i) e -> p c e i", i=4),
-                    in_=raw[:, :, cut:].rearrange("p e (c i) -> p c e i", i=4),
-                )
+        def round_x(u):
+            for c, (lo, hi) in enumerate(spans(X_CHUNKS[u])):
+                cut = X_ON_VECTOR[u][c]
+                for copy, first, last in ((nc.vector.tensor_copy, 0, cut), (nc.scalar.copy, cut, hi - lo)):
+                    if first < last:
+                        copy(
+                            out=x_pairs[u][:, lo + first : lo + last, :].rearrange("p (c i) e -> p c e i", i=RUN),
+                            in_=x_raw[u, c][:, :, first:last].rearrange("p e (c i) -> p c e i", i=RUN),
+                        )
 
-        def gather(u, n):
-            lo, hi = spans(PICK_PIECES)[n]
+        def gather_pairs(u, n):
             window = x_pairs[u][:].rearrange("p c e -> p (c e)").bitcast(U32)
-            nc.vector.tensor_copy(gathered[n][:, u, :], window.indirect(offs_sb[:, lo // 16 : hi // 16]))
+            entries = offs_sb[:, n * PIECE // STRIPE : (n + 1) * PIECE // STRIPE]
+            nc.vector.tensor_copy(gathered[n][:, u, :], window.indirect(entries))
 
         x_woven = {}
-        x_halves = []
 
-        def weave(n):
-            lo, hi = spans(PICK_PIECES)[n]
-            if n < 3:
-                x_halves.append(keep.tile([P, HALF, 2], U32, name="x_woven%d" % n, tag=("turn0", "w1_raw1", "turn1")[n], align_bytes=64))
-            x_woven[n] = x_halves[-1][:, (n // 3) * (hi - lo) : (n // 3 + 1) * (hi - lo), :]
-            if n < 2:
-                nc.scalar.copy(
-                    out=x_woven[n].rearrange("p (c i) u -> p c u i", i=2),
-                    in_=gathered[n][:].rearrange("p u (c i) -> p c u i", i=2),
-                )
-            else:
-                nc.vector.tensor_copy(
-                    out=x_woven[n].bitcast(I32).rearrange("p (c i) u -> p c u i", i=2),
-                    in_=gathered[n][:].bitcast(I32).rearrange("p u (c i) -> p c u i", i=2),
-                )
+        def weave(n, copy, word, target):
+            x_woven[n] = target
+            copy(
+                out=target.bitcast(word).rearrange("p (c i) u -> p c u i", i=2),
+                in_=gathered[n][:].bitcast(word).rearrange("p u (c i) -> p c u i", i=2),
+            )
 
         picked = {}
 
         def quantise_x(n):
-            lo, hi = spans(PICK_PIECES)[n]
-            words = keep.tile([P, hi - lo], U32, name="picked_words%d" % n, align_bytes=64)
-            plane = keep.tile([P, hi - lo], U8, name="picked_plane%d" % n, align_bytes=64)
-            nc.vector.quantize_mx(
-                out=words[:].bitcast(FP8X4), scales=plane[:], in_=x_woven[n].rearrange("p c u -> p (c u)").bitcast(BF16)
-            )
-            picked[n] = (words, plane)
+            picked[n] = quantise("picked%d" % n, x_woven[n].rearrange("p c u -> p (c u)").bitcast(BF16))
 
-        for piece in x_raw:
-            if piece[0] == 0:
-                cast(*piece)
-        for n in range(4):
-            gather(0, n)
-        for piece in x_raw:
-            if piece[0] == 1:
-                cast(*piece)
+        round_x(0)
+        for n in range(PIECES):
+            gather_pairs(0, n)
+        round_x(1)
 
+        w1_woven = [keep.tile([P, 2, P, PACK], BF16, name="w1_woven%d" % u, tag="w1_woven%d" % u, align_bytes=64) for u in range(2)]
         w1_q = []
-        w1_woven = [keep.tile([P, 2, P, PACK], BF16, name="w1_woven%d" % u, tag="turn%d" % (1 + 2 * u), align_bytes=64) for u in range(2)]
 
-        def cast_w1(n):
-            lo, hi = spans(W1_CHUNKS)[n]
+        def round_w1(c):
+            lo, hi = spans(W1_CHUNKS)[c]
             for u in range(2):
                 nc.scalar.copy(
                     out=w1_woven[u][:, :, lo // PACK : hi // PACK, :].rearrange("p e m j -> p m j e"),
-                    in_=w1_raw[n][:].rearrange("p j (m u e) -> p u m j e", u=2, e=2)[:, u],
+                    in_=w1_raw[c][:].rearrange("p j (m u e) -> p u m j e", u=2, e=2)[:, u],
                 )
 
         def quantise_w1(u):
-            words = keep.tile([P, 2 * P], U32, name="w1_words%d" % u, align_bytes=64)
-            plane = keep.tile([P, 2 * P], U8, name="w1_plane%d" % u, align_bytes=64)
-            nc.vector.quantize_mx(out=words[:].bitcast(FP8X4), scales=plane[:], in_=w1_woven[u][:].rearrange("p e m j -> p (e m j)"))
+            codes, scales = quantise("w1_%d" % u, w1_woven[u][:].rearrange("p e m j -> p (e m j)"))
             for e in range(2):
-                w1_q.append((words[:, e * P : (e + 1) * P], plane[:, e * P : (e + 1) * P]))
+                w1_q.append((codes[:, e * P : (e + 1) * P], scales[:, e * P : (e + 1) * P]))
 
-        h_window = [keep.tile([P, S], F32, name="h_window%d" % t) for t in range(PACK)]
-        h_rest = keep.tile([P, PACK, S - ON_PE], F32, name="h_rest")
-
-        def bank(b, shape):
-            return psum.tile(shape, F32, name="bank%d" % b, tag="bank%d" % b)
-
-        def first_product(t, pieces, b):
-            acc = bank(b, [P, BANK])
-            first = spans(PICK_PIECES)[pieces[0]][0]
-            for n in pieces:
-                lo, hi = spans(PICK_PIECES)[n]
-                nc.tensor.matmul_mx(
-                    out=acc[:, lo - first : hi - first],
-                    lhsT=w1_q[t][0].bitcast(FP8X4), lhsT_scale=w1_q[t][1],
-                    rhs=picked[n][0][:].bitcast(FP8X4), rhs_scale=picked[n][1][:],
-                    start=True, stop=True,
-                )
-            last = spans(PICK_PIECES)[pieces[-1]][1]
-            nc.scalar.activation(h_window[t][:, first:last], acc[:, 0 : last - first], GELU, bias=no_bias[:])
-
-        def second_copy(t):
-            nc.sync.dma_start(out=h_rest[:, t, :], in_=h_window[t][:, ON_PE : S])
-
-        cast_w1(0)
-        gather(1, 0)
-        weave(0)
-        cast_w1(1)
-        gather(1, 1)
-        weave(1)
-        gather(1, 2)
-        gather(1, 3)
+        round_w1(0)
+        gather_pairs(1, 0)
+        weave(0, nc.scalar.copy, U32, keep.tile([P, PIECE, 2], U32, name="x_woven0", align_bytes=64)[:])
+        round_w1(1)
+        gather_pairs(1, 1)
+        weave(1, nc.scalar.copy, U32, keep.tile([P, PIECE, 2], U32, name="x_woven1", tag="w1_raw1", align_bytes=64)[:])
+        gather_pairs(1, 2)
+        gather_pairs(1, 3)
         quantise_x(0)
         quantise_w1(0)
-        weave(2)
-        weave(3)
-        quantise_x(2)
-        quantise_x(3)
-        quantise_x(1)
+        x_woven_late = keep.tile([P, 2, PIECE, 2], U32, name="x_woven_late", tag="w1_woven0", align_bytes=64)
+        for n in (2, 3):
+            weave(n, nc.vector.tensor_copy, I32, x_woven_late[:, n - 2])
+        for n in (2, 3, 1):
+            quantise_x(n)
         quantise_w1(1)
-        first_product(0, [0], 0)
-        first_product(0, [2], 1)
-        first_product(0, [3], 2)
-        first_product(0, [1], 3)
-        second_copy(0)
-        first_product(1, [0, 1], 4)
-        first_product(1, [2, 3], 1)
-        second_copy(1)
-        for t in range(2, PACK):
-            first_product(t, [0, 1], 2 * t + 1)
-            first_product(t, [2, 3], 6 if t == 2 else 0)
-            second_copy(t)
 
-        taken = {}
-        sums = {}
-        back_banks = (7, 0, 2)
-        sum_banks = ((2, 3, 4), (1, 5, 6))
+        h_plane = [keep.tile([P, S], F32, name="h_plane%d" % t) for t in range(PACK)]
+        h_rest = keep.tile([P, PACK, NODE_PARTS[1]], F32, name="h_rest")
 
-        def take(t, n):
-            lo, hi = spans(TAKES)[n]
-            nc.vector.tensor_tensor(taken[n][:, t, :], h_window[t][:].indirect(par_sb[:, lo // 16 : hi // 16]), share_sb[n][:], MULT)
+        def first_product(t, first, count, number):
+            acc = bank(number, [P, count, PIECE])
+            for n in range(count):
+                codes, scales = picked[first + n]
+                nc.tensor.matmul_mx(
+                    out=acc[:, n, :],
+                    lhsT=w1_q[t][0].bitcast(FP8X4),
+                    lhsT_scale=w1_q[t][1],
+                    rhs=codes[:].bitcast(FP8X4),
+                    rhs_scale=scales[:],
+                    start=True,
+                    stop=True,
+                )
+            nodes = slice(first * PIECE, (first + count) * PIECE)
+            nc.scalar.activation(h_plane[t][:, nodes], acc[:].rearrange("p n c -> p (n c)"), GELU, bias=no_bias[:])
 
-        def sum_up(t):
+        def copy_rest(t):
+            nc.sync.dma_start(out=h_rest[:, t, :], in_=h_plane[t][:, ON_TENSOR:S])
+
+        for number, n in enumerate((0, 2, 3, 1)):
+            first_product(0, n, 1, number)
+        copy_rest(0)
+        for t, numbers in ((1, (4, 1)), (2, (5, 6)), (3, (7, 0))):
+            for half in range(2):
+                first_product(t, 2 * half, 2, numbers[half])
+            copy_rest(t)
+
+        taken, sums, back, z_woven = {}, {}, {}, {}
+
+        def take(t, part):
+            first, last = spans(NODE_PARTS)[part]
+            step = PIECE if t == PACK - 1 else last - first
+            for lo in range(first, last, step):
+                nodes = slice(lo - first, lo - first + step)
+                entries = par_sb[:, lo // STRIPE : (lo + step) // STRIPE]
+                nc.vector.tensor_tensor(taken[part][:, t, nodes], h_plane[t][:].indirect(entries), share_sb[part][:, nodes], MULT)
+
+        def add_on_tensor(t):
             u, e = divmod(t, 2)
-            for j in range(ON_PE // P):
-                n, jj = divmod(j, 2)
-                if (u, n) not in sums:
-                    sums[u, n] = bank(sum_banks[u][n], [P, 2, 2, P])
-                cols = slice(j * P, (j + 1) * P)
-                nc.tensor.matmul(sums[u, n][:, jj, e, :], h_window[t][:, cols], identity[:], start=True, stop=False, is_transpose=True)
-                nc.tensor.matmul(sums[u, n][:, jj, e, :], taken[0][:, t, cols], identity[:], start=False, stop=True, is_transpose=True)
+            for n in range(ON_TENSOR // PIECE):
+                if e == 0:
+                    sums[u, n] = bank(SUM_BANKS[u][n], [P, 2, 2, P])
+                for block in range(2):
+                    nodes = slice(n * PIECE + block * P, n * PIECE + (block + 1) * P)
+                    target = sums[u, n][:, block, e, :]
+                    nc.tensor.matmul(target, h_plane[t][:, nodes], identity[:], start=True, stop=False, is_transpose=True)
+                    nc.tensor.matmul(target, taken[0][:, t, nodes], identity[:], start=False, stop=True, is_transpose=True)
 
-        z_woven = {}
+        def turn_back(u, n):
+            if u == 0:
+                back[n] = bank(BACK_BANKS[n], [P, 2, 2, P])
+            z_pairs = keep.tile([P, 2, P, 2], BF16, name="z_pairs%d_%d" % (u, n), align_bytes=64)
+            nc.scalar.copy(out=z_pairs[:], in_=sums[u, n][:].rearrange("q b e p -> q b p e"))
+            words = z_pairs[:].rearrange("q b p e -> q (b p e)").bitcast(F32)
+            for block in range(2):
+                nc.tensor.transpose(back[n][:, block, u, :], words[:, block * P : (block + 1) * P], identity[:])
+            if u == 1:
+                z_woven[n] = keep.tile([P, PIECE, PACK], BF16, name="z_woven%d" % n, tag="z_woven%d" % n, align_bytes=64)
+                nc.scalar.copy(
+                    out=z_woven[n][:].rearrange("p c t -> p (c t)").bitcast(F32).rearrange("p (b c u) -> p b c u", b=2, u=2),
+                    in_=back[n][:].rearrange("p b u c -> p b c u"),
+                )
 
-        def woven_tile(n):
+        def add_on_vector(n, behind):
             lo, hi = spans(Z_PIECES)[n]
-            if n not in z_woven:
-                z_woven[n] = keep.tile([P, hi - lo, PACK], BF16, name="z_woven%d" % n, tag=("z0", "z1", "turned1_0", "z1", "turned1_0")[n], align_bytes=64)
-            return z_woven[n]
-
-        def add(n):
-            first, hi = spans(Z_PIECES)[n]
-            lo = max(first, ON_PE)
+            nodes = slice(lo - ON_TENSOR, hi - ON_TENSOR)
+            z_woven[n] = keep.tile([P, hi - lo, PACK], BF16, name="z_woven%d" % n, tag="z_woven%d" % behind, align_bytes=64)
             nc.vector.tensor_tensor(
-                woven_tile(n)[:, lo - first :, :].rearrange("p (c i) t -> p c t i", i=4),
-                taken[1][:, :, lo - ON_PE : hi - ON_PE].rearrange("p t (c i) -> p c t i", i=4),
-                h_rest[:, :, lo - ON_PE : hi - ON_PE].rearrange("p t (c i) -> p c t i", i=4),
+                z_woven[n][:].rearrange("p (c i) t -> p c t i", i=RUN),
+                taken[1][:, :, nodes].rearrange("p t (c i) -> p c t i", i=RUN),
+                h_rest[:, :, nodes].rearrange("p t (c i) -> p c t i", i=RUN),
                 ADD,
             )
 
-        back = {}
+        out_rows = out.rearrange("(r p) c -> p r c", p=P)
 
-        def turn_back(u, n):
+        def second_product(n, copy):
             lo, hi = spans(Z_PIECES)[n]
-            count = (min(hi, ON_PE) - lo) // P
-            if u == 0:
-                back[n] = bank(back_banks[n], [P, count, 2, P])
-            turned = keep.tile([P, count, P, 2], BF16, name="turned%d_%d" % (u, n), tag="turned%d_%d" % (u, n), align_bytes=64)
-            nc.scalar.copy(out=turned[:], in_=sums[u, n][:, 0:count].rearrange("q j e p -> q j p e"))
-            pairs = turned[:].rearrange("q j p e -> q (j p e)").bitcast(F32)
-            for jj in range(count):
-                nc.tensor.transpose(back[n][:, jj, u, :], pairs[:, jj * P : (jj + 1) * P], identity[:])
-            if u == 1:
-                nc.scalar.copy(
-                    out=woven_tile(n)[:, 0 : count * P, :].rearrange("p c t -> p (c t)").bitcast(F32).rearrange("p (j c u) -> p j c u", j=count, u=2),
-                    in_=back[n][:].rearrange("p j u c -> p j c u"),
-                )
-
-        out_rows = out.rearrange("(u p) c -> p u c", p=P)
-
-        def second_product(n, banks, engines):
-            lo, hi = spans(Z_PIECES)[n]
-            width = hi - lo
-            words = keep.tile([P, width], U32, name="z_words%d" % n, align_bytes=64)
-            plane = keep.tile([P, width], U8, name="z_plane%d" % n, align_bytes=64)
-            nc.vector.quantize_mx(out=words[:].bitcast(FP8X4), scales=plane[:], in_=z_woven[n][:].rearrange("p c t -> p (c t)"))
-            result = keep.tile([P, N // P, width], F32, name="result%d" % n)
-            accs = [bank(b, [P, N // P, width]) for b in banks]
-            for u in range(N // P):
+            codes, scales = quantise("z%d" % n, z_woven[n][:].rearrange("p c t -> p (c t)"))
+            result = keep.tile([P, N // P, hi - lo], F32, name="result%d" % n)
+            acc = bank(OUT_BANKS[n], [P, N // P, hi - lo])
+            for r in range(N // P):
                 nc.tensor.matmul_mx(
-                    out=accs[u % len(banks)][:, u, :],
-                    lhsT=w2_codes[:, u * P : (u + 1) * P].bitcast(FP8X4), lhsT_scale=w2_plane[:, u * P : (u + 1) * P],
-                    rhs=words[:].bitcast(FP8X4), rhs_scale=plane[:],
-                    start=True, stop=True,
+                    out=acc[:, r, :],
+                    lhsT=w2_codes[:, r * P : (r + 1) * P].bitcast(FP8X4),
+                    lhsT_scale=w2_bytes[:, r * P : (r + 1) * P],
+                    rhs=codes[:].bitcast(FP8X4),
+                    rhs_scale=scales[:],
+                    start=True,
+                    stop=True,
                 )
-            if len(banks) == 1:
-                engines[0](out=result[:], in_=accs[0][:])
-            else:
-                for u in range(N // P):
-                    engines[u](out=result[:, u, :], in_=accs[u][:, u, :])
+            copy(out=result[:], in_=acc[:])
             nc.sync.dma_start(out=out_rows[:, :, lo:hi], in_=result[:])
 
-        taken[0] = keep.tile([P, PACK, TAKES[0]], F32, name="taken0")
-        for t in range(PACK):
-            take(t, 0)
-            sum_up(t)
-            if t % 2 == 1:
-                for n in range(len(back_banks)):
-                    turn_back(t // 2, n)
-        taken[1] = keep.tile([P, PACK, TAKES[1]], F32, name="taken1", tag="share0")
+        taken[0] = keep.tile([P, PACK, NODE_PARTS[0]], F32, name="taken0")
+        for u in range(2):
+            for e in range(2):
+                take(2 * u + e, 0)
+                add_on_tensor(2 * u + e)
+            for n in range(ON_TENSOR // PIECE):
+                turn_back(u, n)
+        taken[1] = keep.tile([P, PACK, NODE_PARTS[1]], F32, name="taken1", tag="share0")
         for t in range(PACK):
             take(t, 1)
-        scalar, vector = nc.scalar.copy, nc.vector.tensor_copy
-        second_product(0, [3], [scalar])
-        add(2)
-        second_product(1, [4], [scalar])
-        second_product(2, [1], [scalar])
-        add(3)
-        add(4)
-        second_product(3, [5], [vector])
-        second_product(4, [6, 7], [scalar, vector])
+        second_product(0, nc.scalar.copy)
+        add_on_vector(3, behind=0)
+        second_product(1, nc.scalar.copy)
+        add_on_vector(4, behind=1)
+        second_product(2, nc.scalar.copy)
+        second_product(3, nc.scalar.copy)
+        second_product(4, nc.vector.tensor_copy)

@@ -27,13 +27,15 @@ PIECES = S // PIECE
 X_CHUNKS = ((1024, 1024), (1024, 512, 512))
 X_ON_VECTOR = ((640, 640), (0, 512, 320))
 W1_CHUNKS = (192, 320)
-ON_TENSOR = 3 * PIECE
+ON_TENSOR = 5 * P
 NODE_PARTS = (ON_TENSOR, S - ON_TENSOR)
 Z_PIECES = (PIECE, PIECE, PIECE, P, P)
+TENSOR_BLOCKS = (2, 2, 1)
 
 SUM_BANKS = ((2, 3, 4), (1, 5, 6))
 BACK_BANKS = (7, 0, 2)
 OUT_BANKS = (3, 4, 1, 5, 6)
+Z_TAGS = ("z_woven0", "z_woven1", "z_pairs1_0", "z_woven1", "z_pairs1_0")
 
 
 def spans(widths):
@@ -197,45 +199,45 @@ def tile_picked_treeup_gelu_e_kernel(tc, xT, w1, w2_words, w2_scales, share, off
         taken, sums, back, z_woven = {}, {}, {}, {}
 
         def take(t, part):
-            first, last = spans(NODE_PARTS)[part]
-            step = PIECE if t == PACK - 1 else last - first
-            for lo in range(first, last, step):
-                nodes = slice(lo - first, lo - first + step)
-                entries = par_sb[:, lo // STRIPE : (lo + step) // STRIPE]
-                nc.vector.tensor_tensor(taken[part][:, t, nodes], h_plane[t][:].indirect(entries), share_sb[part][:, nodes], MULT)
+            lo, hi = spans(NODE_PARTS)[part]
+            entries = par_sb[:, lo // STRIPE : hi // STRIPE]
+            nc.vector.tensor_tensor(taken[part][:, t, :], h_plane[t][:].indirect(entries), share_sb[part][:], MULT)
 
         def add_on_tensor(t):
             u, e = divmod(t, 2)
-            for n in range(ON_TENSOR // PIECE):
+            for n, blocks in enumerate(TENSOR_BLOCKS):
                 if e == 0:
-                    sums[u, n] = bank(SUM_BANKS[u][n], [P, 2, 2, P])
-                for block in range(2):
+                    sums[u, n] = bank(SUM_BANKS[u][n], [P, blocks, 2, P])
+                for block in range(blocks):
                     nodes = slice(n * PIECE + block * P, n * PIECE + (block + 1) * P)
                     target = sums[u, n][:, block, e, :]
                     nc.tensor.matmul(target, h_plane[t][:, nodes], identity[:], start=True, stop=False, is_transpose=True)
                     nc.tensor.matmul(target, taken[0][:, t, nodes], identity[:], start=False, stop=True, is_transpose=True)
 
         def turn_back(u, n):
+            blocks = TENSOR_BLOCKS[n]
             if u == 0:
-                back[n] = bank(BACK_BANKS[n], [P, 2, 2, P])
-            z_pairs = keep.tile([P, 2, P, 2], BF16, name="z_pairs%d_%d" % (u, n), align_bytes=64)
+                back[n] = bank(BACK_BANKS[n], [P, blocks, 2, P])
+            z_pairs = keep.tile([P, blocks, P, 2], BF16, name="z_pairs%d_%d" % (u, n), tag="z_pairs%d_%d" % (u, n), align_bytes=64)
             nc.scalar.copy(out=z_pairs[:], in_=sums[u, n][:].rearrange("q b e p -> q b p e"))
             words = z_pairs[:].rearrange("q b p e -> q (b p e)").bitcast(F32)
-            for block in range(2):
+            for block in range(blocks):
                 nc.tensor.transpose(back[n][:, block, u, :], words[:, block * P : (block + 1) * P], identity[:])
             if u == 1:
-                z_woven[n] = keep.tile([P, PIECE, PACK], BF16, name="z_woven%d" % n, tag="z_woven%d" % n, align_bytes=64)
+                z_woven[n] = keep.tile([P, PIECE, PACK], BF16, name="z_woven%d" % n, tag=Z_TAGS[n], align_bytes=64)
+                target = z_woven[n][:, 0 : blocks * P, :].rearrange("p c t -> p (c t)").bitcast(F32)
                 nc.scalar.copy(
-                    out=z_woven[n][:].rearrange("p c t -> p (c t)").bitcast(F32).rearrange("p (b c u) -> p b c u", b=2, u=2),
+                    out=target.rearrange("p (b c u) -> p b c u", b=blocks, u=2),
                     in_=back[n][:].rearrange("p b u c -> p b c u"),
                 )
 
-        def add_on_vector(n, behind):
+        def add_on_vector(n):
             lo, hi = spans(Z_PIECES)[n]
-            nodes = slice(lo - ON_TENSOR, hi - ON_TENSOR)
-            z_woven[n] = keep.tile([P, hi - lo, PACK], BF16, name="z_woven%d" % n, tag="z_woven%d" % behind, align_bytes=64)
+            if n not in z_woven:
+                z_woven[n] = keep.tile([P, hi - lo, PACK], BF16, name="z_woven%d" % n, tag=Z_TAGS[n], align_bytes=64)
+            nodes = slice(hi - P - ON_TENSOR, hi - ON_TENSOR)
             nc.vector.tensor_tensor(
-                z_woven[n][:].rearrange("p (c i) t -> p c t i", i=RUN),
+                z_woven[n][:, hi - lo - P :, :].rearrange("p (c i) t -> p c t i", i=RUN),
                 taken[1][:, :, nodes].rearrange("p t (c i) -> p c t i", i=RUN),
                 h_rest[:, :, nodes].rearrange("p t (c i) -> p c t i", i=RUN),
                 ADD,
@@ -266,15 +268,16 @@ def tile_picked_treeup_gelu_e_kernel(tc, xT, w1, w2_words, w2_scales, share, off
             for e in range(2):
                 take(2 * u + e, 0)
                 add_on_tensor(2 * u + e)
-            for n in range(ON_TENSOR // PIECE):
+            for n in range(len(TENSOR_BLOCKS)):
                 turn_back(u, n)
         taken[1] = keep.tile([P, PACK, NODE_PARTS[1]], F32, name="taken1", tag="share0")
         for t in range(PACK):
             take(t, 1)
         second_product(0, nc.scalar.copy)
-        add_on_vector(3, behind=0)
+        add_on_vector(2)
         second_product(1, nc.scalar.copy)
-        add_on_vector(4, behind=1)
         second_product(2, nc.scalar.copy)
+        add_on_vector(3)
+        add_on_vector(4)
         second_product(3, nc.scalar.copy)
         second_product(4, nc.vector.tensor_copy)

from contextlib import ExitStack

import concourse.mybir as mybir
from concourse.masks import make_identity

K, T, S, H, N = 512, 2048, 1024, 512, 256
FLOPS = 2 * S * H * (K + N)

F32 = mybir.dt.float32
BF16 = mybir.dt.bfloat16
I32 = mybir.dt.int32
U32 = mybir.dt.uint32
U16 = mybir.dt.uint16
U8 = mybir.dt.uint8
FP8X4 = mybir.dt.float8_e4m3fn_x4
GELU = mybir.ActivationFunctionType.Gelu_apprx_tanh
MULT = mybir.AluOpType.mult
ADD = mybir.AluOpType.add

P = 128
PACK = 4
STRIPE = 16
RUN = 4
PIECE = 256
PIECES = S // PIECE

X_CHUNKS = ((1024, 1024), (1024, 512, 512))
X_ON_VECTOR = ((640, 640), (0, 512, 320))
W1_CHUNKS = (192, 320)
ON_TENSOR = 5 * P
NODE_PARTS = (ON_TENSOR, S - ON_TENSOR)
Z_PIECES = (PIECE, PIECE, PIECE, P, P)
TENSOR_BLOCKS = (2, 2, 1)

SUM_BANKS = ((2, 3, 4), (1, 5, 6))
BACK_BANKS = (7, 0, 2)
OUT_BANKS = (3, 4, 1, 5, 6)
Z_TAGS = ("z_woven0", "z_woven1", "z_pairs1_0", "z_woven1", "z_pairs1_0")


def spans(widths):
    found, start = [], 0
    for width in widths:
        found.append((start, start + width))
        start = start + width
    return found


def tile_picked_treeup_gelu_e_kernel(tc, xT, w1, w2_words, w2_scales, share, offs, par, out):
    nc = tc.nc
    with ExitStack() as ctx:
        keep = ctx.enter_context(tc.tile_pool(name="keep", bufs=1))
        psum = ctx.enter_context(tc.psum_pool(name="psum", bufs=1))

        def bank(number, shape):
            return psum.tile(shape, F32, name="bank%d" % number, tag="bank%d" % number)

        def quantise(name, woven):
            columns = woven.shape[1] // PACK
            codes = keep.tile([P, columns], U32, name=name + "_codes", align_bytes=64)
            scales = keep.tile([P, columns], U8, name=name + "_scales", align_bytes=64)
            nc.vector.quantize_mx(out=codes[:].bitcast(FP8X4), scales=scales[:], in_=woven)
            return codes, scales

        offs_sb = keep.tile([P, S // STRIPE], U16, name="offs_sb")
        par_sb = keep.tile([P, S // STRIPE], U16, name="par_sb")
        x_rows = xT.rearrange("(p u e) c -> p u e c", u=2, e=2)
        x_raw = {}
        for u in range(2):
            for c, (lo, hi) in enumerate(spans(X_CHUNKS[u])):
                x_raw[u, c] = keep.tile([P, 2, hi - lo], F32, name="x_raw%d_%d" % (u, c))
                nc.sync.dma_start(out=x_raw[u, c][:], in_=x_rows[:, u, :, lo:hi])
                if (u, c) == (0, 0):
                    nc.sync.dma_start(offs_sb[:], offs)
        w1_rows = w1.rearrange("(p j) c -> p j c", j=PACK)
        w1_raw = []
        for c, (lo, hi) in enumerate(spans(W1_CHUNKS)):
            w1_raw.append(keep.tile([P, PACK, hi - lo], F32, name="w1_raw%d" % c, tag="w1_raw%d" % c, align_bytes=64))
            nc.sync.dma_start(out=w1_raw[c][:], in_=w1_rows[:, :, lo:hi])
        nc.sync.dma_start(par_sb[:], par)
        share_sb = []
        for part, (lo, hi) in enumerate(spans(NODE_PARTS)):
            share_sb.append(keep.tile([P, hi - lo], F32, name="share%d" % part, tag="share%d" % part))
            nc.sync.dma_start(out=share_sb[part][:], in_=share[:, lo:hi])
        w2_codes = keep.tile([P, N], I32, name="w2_codes", align_bytes=64)
        nc.sync.dma_start(out=w2_codes[:], in_=w2_words[0].rearrange("p n t -> p (n t)").bitcast(I32))
        w2_bytes = keep.tile([P, N], U8, name="w2_bytes", align_bytes=64)
        nc.vector.memset(w2_bytes[:].bitcast(I32), 0)
        for q in range(4):
            nc.sync.dma_start(out=w2_bytes[32 * q : 32 * q + 4, :].bitcast(I32), in_=w2_scales[0, 4 * q : 4 * q + 4, :].bitcast(I32))

        zero = keep.tile([P, 1], F32, name="zero")
        nc.vector.memset(zero[:], 0.0)
        no_bias = keep.tile([P, 1], F32, name="no_bias")
        nc.scalar.activation(no_bias[:], zero[:], GELU)
        identity = keep.tile([P, P], F32, name="identity")
        make_identity(nc, identity[:])

        x_pairs = [keep.tile([P, T, 2], BF16, name="x_pairs%d" % u) for u in range(2)]
        gathered = [keep.tile([P, 2, PIECE], U32, name="gathered%d" % n) for n in range(PIECES)]

        def round_x(u):
            for c, (lo, hi) in enumerate(spans(X_CHUNKS[u])):
                cut = X_ON_VECTOR[u][c]
                for copy, first, last in ((nc.vector.tensor_copy, 0, cut), (nc.scalar.copy, cut, hi - lo)):
                    if first < last:
                        copy(
                            out=x_pairs[u][:, lo + first : lo + last, :].rearrange("p (c i) e -> p c e i", i=RUN),
                            in_=x_raw[u, c][:, :, first:last].rearrange("p e (c i) -> p c e i", i=RUN),
                        )

        def gather_pairs(u, n):
            window = x_pairs[u][:].rearrange("p c e -> p (c e)").bitcast(U32)
            entries = offs_sb[:, n * PIECE // STRIPE : (n + 1) * PIECE // STRIPE]
            nc.vector.tensor_copy(gathered[n][:, u, :], window.indirect(entries))

        x_woven = {}

        def weave(n, copy, word, target):
            x_woven[n] = target
            copy(
                out=target.bitcast(word).rearrange("p (c i) u -> p c u i", i=2),
                in_=gathered[n][:].bitcast(word).rearrange("p u (c i) -> p c u i", i=2),
            )

        picked = {}

        def quantise_x(n):
            picked[n] = quantise("picked%d" % n, x_woven[n].rearrange("p c u -> p (c u)").bitcast(BF16))

        round_x(0)
        for n in range(PIECES):
            gather_pairs(0, n)
        round_x(1)

        w1_woven = [keep.tile([P, 2, P, PACK], BF16, name="w1_woven%d" % u, tag="w1_woven%d" % u, align_bytes=64) for u in range(2)]
        w1_q = []

        def round_w1(c):
            lo, hi = spans(W1_CHUNKS)[c]
            for u in range(2):
                nc.scalar.copy(
                    out=w1_woven[u][:, :, lo // PACK : hi // PACK, :].rearrange("p e m j -> p m j e"),
                    in_=w1_raw[c][:].rearrange("p j (m u e) -> p u m j e", u=2, e=2)[:, u],
                )

        def quantise_w1(u):
            codes, scales = quantise("w1_%d" % u, w1_woven[u][:].rearrange("p e m j -> p (e m j)"))
            for e in range(2):
                w1_q.append((codes[:, e * P : (e + 1) * P], scales[:, e * P : (e + 1) * P]))

        round_w1(0)
        gather_pairs(1, 0)
        weave(0, nc.scalar.copy, U32, keep.tile([P, PIECE, 2], U32, name="x_woven0", align_bytes=64)[:])
        round_w1(1)
        gather_pairs(1, 1)
        weave(1, nc.scalar.copy, U32, keep.tile([P, PIECE, 2], U32, name="x_woven1", tag="w1_raw1", align_bytes=64)[:])
        gather_pairs(1, 2)
        gather_pairs(1, 3)
        quantise_x(0)
        quantise_w1(0)
        x_woven_late = keep.tile([P, 2, PIECE, 2], U32, name="x_woven_late", tag="w1_woven0", align_bytes=64)
        for n in (2, 3):
            weave(n, nc.vector.tensor_copy, I32, x_woven_late[:, n - 2])
        for n in (2, 3, 1):
            quantise_x(n)
        quantise_w1(1)

        h_plane = [keep.tile([P, S], F32, name="h_plane%d" % t) for t in range(PACK)]
        h_rest = keep.tile([P, PACK, NODE_PARTS[1]], F32, name="h_rest")

        def first_product(t, first, count, number):
            acc = bank(number, [P, count, PIECE])
            for n in range(count):
                codes, scales = picked[first + n]
                nc.tensor.matmul_mx(
                    out=acc[:, n, :],
                    lhsT=w1_q[t][0].bitcast(FP8X4),
                    lhsT_scale=w1_q[t][1],
                    rhs=codes[:].bitcast(FP8X4),
                    rhs_scale=scales[:],
                    start=True,
                    stop=True,
                )
            nodes = slice(first * PIECE, (first + count) * PIECE)
            nc.scalar.activation(h_plane[t][:, nodes], acc[:].rearrange("p n c -> p (n c)"), GELU, bias=no_bias[:])

        def copy_rest(t):
            nc.sync.dma_start(out=h_rest[:, t, :], in_=h_plane[t][:, ON_TENSOR:S])

        for number, n in enumerate((0, 2, 3, 1)):
            first_product(0, n, 1, number)
        copy_rest(0)
        for t, numbers in ((1, (4, 1)), (2, (5, 6)), (3, (7, 0))):
            for half in range(2):
                first_product(t, 2 * half, 2, numbers[half])
            copy_rest(t)

        taken, sums, back, z_woven = {}, {}, {}, {}

        def take(t, part):
            lo, hi = spans(NODE_PARTS)[part]
            entries = par_sb[:, lo // STRIPE : hi // STRIPE]
            nc.vector.tensor_tensor(taken[part][:, t, :], h_plane[t][:].indirect(entries), share_sb[part][:], MULT)

        def add_on_tensor(t):
            u, e = divmod(t, 2)
            for n, blocks in enumerate(TENSOR_BLOCKS):
                if e == 0:
                    sums[u, n] = bank(SUM_BANKS[u][n], [P, blocks, 2, P])
                for block in range(blocks):
                    nodes = slice(n * PIECE + block * P, n * PIECE + (block + 1) * P)
                    target = sums[u, n][:, block, e, :]
                    nc.tensor.matmul(target, h_plane[t][:, nodes], identity[:], start=True, stop=False, is_transpose=True)
                    nc.tensor.matmul(target, taken[0][:, t, nodes], identity[:], start=False, stop=True, is_transpose=True)

        def turn_back(u, n):
            blocks = TENSOR_BLOCKS[n]
            if u == 0:
                back[n] = bank(BACK_BANKS[n], [P, blocks, 2, P])
            z_pairs = keep.tile([P, blocks, P, 2], BF16, name="z_pairs%d_%d" % (u, n), tag="z_pairs%d_%d" % (u, n), align_bytes=64)
            nc.scalar.copy(out=z_pairs[:], in_=sums[u, n][:].rearrange("q b e p -> q b p e"))
            words = z_pairs[:].rearrange("q b p e -> q (b p e)").bitcast(F32)
            for block in range(blocks):
                nc.tensor.transpose(back[n][:, block, u, :], words[:, block * P : (block + 1) * P], identity[:])
            if u == 1:
                z_woven[n] = keep.tile([P, PIECE, PACK], BF16, name="z_woven%d" % n, tag=Z_TAGS[n], align_bytes=64)
                target = z_woven[n][:, 0 : blocks * P, :].rearrange("p c t -> p (c t)").bitcast(F32)
                nc.scalar.copy(
                    out=target.rearrange("p (b c u) -> p b c u", b=blocks, u=2),
                    in_=back[n][:].rearrange("p b u c -> p b c u"),
                )

        def add_on_vector(n):
            lo, hi = spans(Z_PIECES)[n]
            if n not in z_woven:
                z_woven[n] = keep.tile([P, hi - lo, PACK], BF16, name="z_woven%d" % n, tag=Z_TAGS[n], align_bytes=64)
            nodes = slice(hi - P - ON_TENSOR, hi - ON_TENSOR)
            nc.vector.tensor_tensor(
                z_woven[n][:, hi - lo - P :, :].rearrange("p (c i) t -> p c t i", i=RUN),
                taken[1][:, :, nodes].rearrange("p t (c i) -> p c t i", i=RUN),
                h_rest[:, :, nodes].rearrange("p t (c i) -> p c t i", i=RUN),
                ADD,
            )

        out_rows = out.rearrange("(r p) c -> p r c", p=P)

        def second_product(n, copy):
            lo, hi = spans(Z_PIECES)[n]
            codes, scales = quantise("z%d" % n, z_woven[n][:].rearrange("p c t -> p (c t)"))
            result = keep.tile([P, N // P, hi - lo], F32, name="result%d" % n)
            acc = bank(OUT_BANKS[n], [P, N // P, hi - lo])
            for r in range(N // P):
                nc.tensor.matmul_mx(
                    out=acc[:, r, :],
                    lhsT=w2_codes[:, r * P : (r + 1) * P].bitcast(FP8X4),
                    lhsT_scale=w2_bytes[:, r * P : (r + 1) * P],
                    rhs=codes[:].bitcast(FP8X4),
                    rhs_scale=scales[:],
                    start=True,
                    stop=True,
                )
            copy(out=result[:], in_=acc[:])
            nc.sync.dma_start(out=out_rows[:, :, lo:hi], in_=result[:])

        taken[0] = keep.tile([P, PACK, NODE_PARTS[0]], F32, name="taken0")
        for u in range(2):
            for e in range(2):
                take(2 * u + e, 0)
                add_on_tensor(2 * u + e)
            for n in range(len(TENSOR_BLOCKS)):
                turn_back(u, n)
        taken[1] = keep.tile([P, PACK, NODE_PARTS[1]], F32, name="taken1", tag="share0")
        for t in range(PACK):
            take(t, 1)
        second_product(0, nc.scalar.copy)
        add_on_vector(2)
        second_product(1, nc.scalar.copy)
        second_product(2, nc.scalar.copy)
        add_on_vector(3)
        add_on_vector(4)
        second_product(3, nc.scalar.copy)
        second_product(4, nc.vector.tensor_copy)
